import numpy as np
import ml_dtypes


def mxq(x, axis, fmt="e4m3"):
    dtype, down = {"e4m3": (ml_dtypes.float8_e4m3fn, 7), "e5m2": (ml_dtypes.float8_e5m2, 14)}[fmt]
    v = np.moveaxis(np.asarray(x, np.float32).astype(ml_dtypes.bfloat16).astype(np.float64), axis, -1)
    blocks = v.reshape(v.shape[:-1] + (-1, 32))
    amax = np.abs(blocks).max(-1, keepdims=True)
    byte = np.maximum(np.where(amax > 0, np.frexp(amax)[1] - 1 + 127, 0) - down, 1)
    scale = np.exp2(byte - 127.0)
    codes = (blocks / scale).astype(np.float32).astype(dtype).astype(np.float64)
    return np.moveaxis((codes * scale).reshape(v.shape), -1, axis)


WIDE = False


def mx_kscale(k):
    if not WIDE:
        return np.ones(k)
    levels = np.array([10, -10, 5, -5, 0])
    if k % 512:
        return np.exp2(np.random.permutation(np.resize(levels, k // 32))).repeat(32)
    a = np.empty((k // 512, 16))
    for p in range(k // 512):
        a[p, :8] = np.random.permutation(np.resize(levels, 8))
        for g in range(8):
            far = levels[np.abs(levels - a[p, g]) >= 10]
            a[p, g + 8] = far[np.random.randint(len(far))]
    return np.exp2(a.ravel()).repeat(32)


BF16 = ml_dtypes.bfloat16


def bf(x):
    return np.asarray(x, np.float32).astype(BF16)


def f64(x):
    return np.asarray(x).astype(np.float64)


E2M1 = np.array([0.0, 0.5, 1.0, 1.5, 2.0, 3.0, 4.0, 6.0, -0.0, -0.5, -1.0, -1.5, -2.0, -3.0, -4.0, -6.0])


def pack_weight(w, fmt):
    k, n = w.shape
    w = f64(bf(w)).reshape(k // 32, 32, n)
    amax = np.abs(w).max(1)
    if fmt == "e4m3":
        byte = np.frexp(amax)[1] - 1 + 127 - 7
    else:
        mant, ex = np.frexp(amax / 6.0)
        byte = np.where(mant > 0.5, ex, ex - 1) + 127
    byte = np.clip(np.where(amax > 0, byte, 1), 1, 254)
    scaled = (w * np.exp2(127.0 - byte)[:, None, :]).reshape(k, n).astype(np.float32)
    by_word = np.ascontiguousarray(scaled.reshape(k // 512, 128, 4, n).transpose(0, 1, 3, 2))
    if fmt == "e4m3":
        words = by_word.astype(ml_dtypes.float8_e4m3fn).view(np.uint8)
    else:
        c = by_word.astype(ml_dtypes.float4_e2m1fn).view(np.uint8) & 0xF
        words = c[..., 0::2] | (c[..., 1::2] << 4)
    return np.ascontiguousarray(words), np.ascontiguousarray(byte.astype(np.uint8).reshape(k // 512, 16, n))


def unpack_weight(words, scales, fmt):
    g, p, n, _ = words.shape
    if fmt == "e4m3":
        vals = np.ascontiguousarray(words).view(ml_dtypes.float8_e4m3fn).astype(np.float64)
    else:
        nib = np.empty((g, p, n, 4), np.uint8)
        nib[..., 0::2] = words & 0xF
        nib[..., 1::2] = words >> 4
        vals = E2M1[nib]
    vals = vals * np.repeat(np.exp2(scales.astype(np.float64) - 127.0), 8, axis=1)[..., None]
    return vals.transpose(0, 1, 3, 2).reshape(g * 512, n)
def pack4(w):
    words, scales = pack_weight(w, "e2m1")
    return words.reshape(words.shape[0], 128, -1), scales


def unpack4(words, scales):
    return unpack_weight(words.reshape(words.shape[0], 128, -1, 2), scales, "e2m1")


E4M3FN = np.array([(-1.0 if i & 128 else 1.0) * ((1.0 + (i & 7) / 8.0) * 2.0 ** (((i >> 3) & 15) - 7) if i & 120 else (i & 7) * 2.0 ** -9) for i in range(256)])


def e4m3fn_bytes(y):
    return np.clip(np.asarray(y, np.float64), -448.0, 448.0).astype(np.float32).astype(ml_dtypes.float8_e4m3fn).view(np.uint8)


def e4m3fn_values(b):
    return E4M3FN[b]


T, D, V, B = 1024, 1024, 2048, 128


def setup_inputs():
    s, t = mx_kscale(D), mx_kscale(V)
    head = 2 * np.random.standard_normal((V, D)) / np.sqrt(D) / t[:, None]
    X = np.random.standard_normal((T, D)) * s
    X_scale = (np.abs(X.reshape(T, D // B, B)).max(2) / 448).astype(np.float32)
    X_bytes = e4m3fn_bytes(X / np.repeat(f64(X_scale), B, 1))
    U_words, U_scales = pack4(head.T / s[:, None])
    W_scale = (np.abs(head.reshape(V // B, B, D // B, B)).max((1, 3)) / 448).astype(np.float32)
    W_bytes = e4m3fn_bytes(head / np.repeat(np.repeat(f64(W_scale), B, 0), B, 1))
    a = bf((1 + 0.1 * np.random.standard_normal(V)) * t)
    y = bf(np.eye(V)[np.random.randint(0, V, T)])
    return {"X_bytes": X_bytes, "X_scale": X_scale, "U_words": U_words, "U_scales": U_scales,
            "W_bytes": W_bytes, "W_scale": W_scale, "a": a, "y": y}


def reference(X_bytes, X_scale, U_words, U_scales, W_bytes, W_scale, a, y):
    X = e4m3fn_values(X_bytes) * np.repeat(f64(X_scale), B, 1)
    W = e4m3fn_values(W_bytes) * np.repeat(np.repeat(f64(W_scale), B, 0), B, 1)
    U = unpack4(U_words, U_scales)
    z = (mxq(X, 1, "e4m3") @ U) * f64(a)
    prob = 1 / (1 + np.exp(-z))
    e = (prob - f64(y)) * f64(a)
    return mxq(e, 1, "e4m3") @ mxq(W, 0, "e4m3")

from contextlib import ExitStack

import concourse.mybir as mybir
from concourse.masks import make_identity

T, D, V = 1024, 1024, 2048
FLOPS = 2 * 2 * T * D * V

F32 = mybir.dt.float32
BF16 = mybir.dt.bfloat16
I32 = mybir.dt.int32
U32 = mybir.dt.uint32
U8 = mybir.dt.uint8
F8 = mybir.dt.float8_e4m3fn
FP8X4 = mybir.dt.float8_e4m3fn_x4
FP4X4 = mybir.dt.float4_e2m1fn_x4
ACT = mybir.ActivationFunctionType
ALU = mybir.AluOpType

P = 128
NH = 2
NG = 4
UNITS = NH * NG
LEAD = 2


def tile_sigmoid_crossentropy_hidden_gradient_d6_kernel(
    tc, X_bytes, X_scale, U_words, U_scales, W_bytes, W_scale, a, y, out
):
    nc = tc.nc
    with ExitStack() as ctx:
        keep = ctx.enter_context(tc.tile_pool(name="keep", bufs=1))
        work = ctx.enter_context(tc.tile_pool(name="work", bufs=2))
        psum = ctx.enter_context(tc.psum_pool(name="psum", bufs=2))
        ctx.enter_context(tc.manual_schedule())

        us_raw = keep.tile([P, 2, V], U8, align_bytes=64, name="us_raw")
        nc.vector.memset(us_raw[:].rearrange("p s v -> p (s v)").bitcast(I32), 0)
        warm = keep.tile([P, 1], F32, name="warm")
        nc.vector.memset(warm[:], 0.0)
        warm_out = keep.tile([P, 1], F32, name="warm_out")
        ident = keep.tile([P, P], F32, name="ident")
        make_identity(nc, ident[:])

        xs = keep.tile([P, 8, 8], F32, name="xs")
        nc.scalar.dma_start(out=xs[:], in_=X_scale.rearrange("(i p) j -> p i j", p=P))
        for q in range(4):
            nc.scalar.dma_start(
                out=us_raw[32 * q : 32 * q + 4, :, :].bitcast(I32),
                in_=U_scales[:, 4 * q : 4 * q + 4, :].rearrange("s r v -> r s v").bitcast(I32),
            )
        a16 = keep.tile([P, NG, 4], BF16, name="a16")
        nc.scalar.dma_start(out=a16[:], in_=a.rearrange("(g p t) -> p g t", p=P, t=4))
        ws_all = keep.tile([P, P], F32, name="ws_all")
        nc.scalar.dma_start(out=ws_all[:], in_=W_scale.rearrange("i j -> (i j)").partition_broadcast(P))
        nc.scalar.activation(warm_out[:], warm[:], ACT.Sigmoid)

        x_view = X_bytes.rearrange("(h i p) d -> h p i d", h=NH, p=P)
        xb = [keep.tile([P, 4, D], U8, align_bytes=64, name="xb%d" % h) for h in range(NH)]
        ur = [keep.tile([P, 2, 1024], U8, align_bytes=64, name="ur%d" % g) for g in range(NG)]
        yt, wb = {}, {}

        def load_x(h, lo, hi):
            nc.sync.dma_start(out=xb[h][:, lo:hi, :], in_=x_view[h][:, lo:hi, :])

        def load_u(g):
            nc.sync.dma_start(
                out=ur[g][:], in_=U_words[:, :, 1024 * g : 1024 * (g + 1)].rearrange("s p b -> p s b")
            )

        y_view = y.rearrange("(h i p) (g v) -> h g p i v", h=NH, p=P, g=NG)

        def load_y(n):
            yt[n] = work.tile([P, 4, 512], BF16, tag="yt", bufs=4, name="yt%d" % n)
            nc.sync.dma_start(out=yt[n][:], in_=y_view[n // NG, n % NG])

        w_view = W_bytes.rearrange("(g p t) (k d) -> g k p t d", p=P, t=4, k=2)

        def load_w(g, k):
            wb[g, k] = keep.tile([P, 4, 512], U8, align_bytes=64, name="wb%d_%d" % (g, k))
            nc.sync.dma_start(out=wb[g, k][:], in_=w_view[g, k])

        load_x(0, 0, 2)
        load_u(0)
        load_x(0, 2, 4)
        load_u(1)
        load_w(0, 0)
        load_y(0)
        load_u(2)
        load_w(1, 0)
        load_x(1, 0, 4)
        load_y(1)
        load_u(3)
        load_w(2, 0)
        load_y(2)
        load_w(3, 0)
        load_y(3)
        for g in range(NG):
            load_w(g, 1)
        for n in range(NG, UNITS):
            load_y(n)

        up = [keep.tile([P, 2, 4, 256], U8, align_bytes=64, name="up%d" % g) for g in range(NG)]
        usp = [keep.tile([P, 2, 4, P], U8, align_bytes=64, name="usp%d" % g) for g in range(NG)]
        xc = [[keep.tile([P, 512], U32, align_bytes=64, name="xc%d_%d" % (h, s)) for s in range(2)] for h in range(NH)]
        xsc = [[keep.tile([P, 512], U8, align_bytes=64, name="xsc%d_%d" % (h, s)) for s in range(2)] for h in range(NH)]
        ec = [keep.tile([P, NG, 512], U32, align_bytes=64, name="ec%d" % h) for h in range(NH)]
        es = [keep.tile([P, NG, 512], U8, align_bytes=64, name="es%d" % h) for h in range(NH)]
        wc = [[keep.tile([P, 512], U32, align_bytes=64, name="wc%d_%d" % (g, k)) for k in range(2)] for g in range(NG)]
        wsc = [[keep.tile([P, 512], U8, align_bytes=64, name="wsc%d_%d" % (g, k)) for k in range(2)] for g in range(NG)]
        af = keep.tile([P, NG, 4], F32, name="af")
        wcol = keep.tile([P, NG, 8], F32, name="wcol")

        def permute_u(g, s):
            nc.vector.tensor_copy(
                out=up[g][:, s].rearrange("p t (m b) -> p t m b", b=2),
                in_=ur[g][:, s].rearrange("p (m t b) -> p t m b", t=4, b=2),
            )

        def permute_us(g):
            nc.vector.tensor_copy(
                out=usp[g][:],
                in_=us_raw[:, :, 512 * g : 512 * (g + 1)].rearrange("p s (m t) -> p s t m", t=4),
            )

        xw, xg = {}, {}

        def widen_x(h, i, on_vector):
            tile = work.tile([P, D], BF16, tag="xw", bufs=4, align_bytes=64, name="xw%d_%d" % (h, i))
            xw[h, i] = tile
            for j in range(8):
                cols = slice(128 * j, 128 * (j + 1))
                src = xb[h][:, i, cols].bitcast(F8)
                scale = xs[:, 4 * h + i, j : j + 1]
                if on_vector:
                    nc.vector.tensor_scalar(out=tile[:, cols], in0=src, scalar1=scale, scalar2=None, op0=ALU.mult)
                else:
                    nc.scalar.activation(tile[:, cols], src, ACT.Copy, scale=scale)

        def turn_x(h, pair, s):
            bank = psum.tile([P, 2, 256], F32, tag="o", bufs=3, name="xt")
            for k in range(2):
                words = xw[h, 2 * pair + k][:].bitcast(F32)
                for u in range(2):
                    nc.tensor.transpose(
                        bank[:, u, 128 * k : 128 * (k + 1)], words[:, 256 * s + u : 256 * (s + 1) : 2], ident[:]
                    )
            if pair == 0:
                xg[h, s] = work.tile([P, 512, 4], BF16, tag="xg", bufs=2, align_bytes=64, name="xg%d_%d" % (h, s))
            dst = xg[h, s][:, 256 * pair : 256 * (pair + 1), :].rearrange("p n t -> p (n t)")
            nc.scalar.copy(
                out=dst.bitcast(F32).rearrange("p (n u) -> p n u", u=2), in_=bank[:].rearrange("p u n -> p n u")
            )

        def quant_x(h, s):
            nc.vector.quantize_mx(
                out=xc[h][s][:].bitcast(FP8X4), scales=xsc[h][s][:], in_=xg[h, s][:].rearrange("p n t -> p (n t)")
            )

        prob, ybank, dif, eb, ww, wi = {}, {}, {}, {}, {}, {}

        def logits(n, t):
            h, g = divmod(n, NG)
            z = psum.tile([P, 512], F32, tag="z", bufs=3, name="z")
            for s in range(2):
                nc.tensor.matmul_mx(
                    out=z[:],
                    lhsT=up[g][:, s, t, :].bitcast(FP4X4),
                    lhsT_scale=usp[g][:, s, t, :],
                    rhs=xc[h][s][:].bitcast(FP8X4),
                    rhs_scale=xsc[h][s][:],
                    start=(s == 0),
                    stop=(s == 1),
                )
            if t == 0:
                prob[n] = work.tile([P, 4, 512], F32, tag="prob", bufs=LEAD + 1, name="prob%d" % n)
            nc.scalar.activation(prob[n][:, t, :], z[:], ACT.Sigmoid, scale=af[:, g, t : t + 1])

        def turn_y(n, u):
            bank = psum.tile([P, 512], F32, tag="y", bufs=2, name="yb")
            ybank[n, u] = bank
            for i in range(4):
                words = yt[n][:, i, :].bitcast(F32)
                nc.tensor.transpose(bank[:, 128 * i : 128 * (i + 1)], words[:, u:256:2], ident[:])

        def subtract(n, u, lo=0, hi=512):
            if n not in dif:
                dif[n] = work.tile([P, 2, 512, 2], F32, tag="dif", bufs=2, name="dif%d" % n)
            nc.vector.tensor_tensor(
                out=dif[n][:, u, lo:hi],
                in0=prob[n][:, 2 * u : 2 * u + 2, lo:hi].rearrange("p e n -> p n e"),
                in1=ybank[n, u][:].bitcast(BF16).rearrange("p (n e) -> p n e", e=2)[:, lo:hi],
                op=ALU.subtract,
            )

        def scale_e(n, k):
            g = n % NG
            if n not in eb:
                eb[n] = work.tile([P, 512, 4], BF16, tag="eb", bufs=2, align_bytes=64, name="eb%d" % n)
            toks = slice(256 * k, 256 * (k + 1))
            nc.vector.tensor_tensor(
                out=eb[n][:, toks, :].rearrange("p n (u e) -> p n u e", u=2),
                in0=dif[n][:, :, toks, :].rearrange("p u n e -> p n u e"),
                in1=af[:, g, :].rearrange("p (u e) -> p u e", u=2).unsqueeze(1).to_broadcast([P, 256, 2, 2]),
                op=ALU.mult,
            )

        def quant_e(n, lo=0, hi=512):
            h, g = divmod(n, NG)
            nc.vector.quantize_mx(
                out=ec[h][:, g, lo:hi].bitcast(FP8X4),
                scales=es[h][:, g, lo:hi],
                in_=eb[n][:, lo:hi, :].rearrange("p n t -> p (n t)"),
            )

        def widen_w(g, k):
            ww[g, k] = work.tile([P, 4, 512], BF16, tag="ww", bufs=3, align_bytes=64, name="ww%d_%d" % (g, k))
            for t in range(0, 4, 2):
                nc.scalar.copy(out=ww[g, k][:, t : t + 2, :], in_=wb[g, k][:, t : t + 2, :].bitcast(F8))

        def weave_w(g, k, j, on_vector=True):
            if (g, k) not in wi:
                wi[g, k] = work.tile([P, 512, 4], BF16, tag="wi", bufs=2, align_bytes=64, name="wi%d_%d" % (g, k))
            cols = slice(128 * j, 128 * (j + 1))
            dst = wi[g, k][:, cols, :]
            src = ww[g, k][:, :, cols].rearrange("p t c -> p c t")
            scale = wcol[:, g, 4 * k + j : 4 * k + j + 1]
            if on_vector:
                nc.vector.tensor_scalar(out=dst, in0=src, scalar1=scale, scalar2=None, op0=ALU.mult)
            else:
                nc.scalar.activation(dst, src, ACT.Copy, scale=scale)

        def quant_w(g, k):
            nc.vector.quantize_mx(
                out=wc[g][k][:].bitcast(FP8X4), scales=wsc[g][k][:], in_=wi[g, k][:].rearrange("p c t -> p (c t)")
            )

        banks = {}

        def gradient(h, i, k, groups, tag, bufs):
            if groups[0] == 0:
                banks[h, i, k] = psum.tile([P, 512], F32, tag=tag, bufs=bufs, name="acc")
            for g in groups:
                nc.tensor.matmul_mx(
                    out=banks[h, i, k][:],
                    lhsT=ec[h][:, g, 128 * i : 128 * (i + 1)].bitcast(FP8X4),
                    lhsT_scale=es[h][:, g, 128 * i : 128 * (i + 1)],
                    rhs=wc[g][k][:].bitcast(FP8X4),
                    rhs_scale=wsc[g][k][:],
                    start=(g == 0),
                    stop=(g == NG - 1),
                )

        def store(h, i, k, on_vector):
            res = work.tile([P, 512], F32, tag="res", bufs=8, name="res")
            if on_vector:
                nc.vector.tensor_copy(out=res[:], in_=banks[h, i, k][:])
            else:
                nc.scalar.copy(out=res[:], in_=banks[h, i, k][:])
            row = 512 * h + 128 * i
            nc.sync.dma_start(out=out[row : row + 128, 512 * k : 512 * (k + 1)], in_=res[:])

        widen_x(0, 0, True)
        widen_x(0, 1, False)
        permute_u(0, 0)
        nc.vector.tensor_copy(out=af[:], in_=a16[:])
        turn_x(0, 0, 0)
        turn_x(0, 0, 1)
        widen_x(0, 2, True)
        widen_x(0, 3, False)
        permute_u(0, 1)
        permute_us(0)
        for q in range(4):
            rows = slice(32 * q, 32 * (q + 1))
            nc.vector.tensor_copy(
                out=wcol[rows], in_=ws_all[rows].rearrange("p (g q j) -> p q g j", g=NG, q=4)[:, q]
            )
        turn_x(0, 1, 0)
        turn_x(0, 1, 1)
        permute_u(1, 0)
        quant_x(0, 0)
        permute_u(1, 1)
        quant_x(0, 1)
        permute_us(1)
        widen_w(0, 0)
        for t in range(4):
            logits(0, t)
        turn_y(0, 0)
        turn_y(0, 1)
        for t in range(4):
            logits(1, t)
        for j in range(4):
            weave_w(0, 0, j)
        permute_u(2, 0)
        permute_u(2, 1)
        permute_us(2)

        fill = [[], [(1, 0)], [(2, 0)], [(3, 0)], [(0, 1), (1, 1)], [(2, 1), (3, 1)], [], []]
        onS = ()
        for n in range(UNITS):
            h, g = divmod(n, NG)
            work_w = [(gg, kk, j) for gg, kk in fill[n] for j in range(4)]
            third = (len(work_w) + 3) // 4
            def weave(q):
                for w in work_w[q * third : (q + 1) * third]:
                    if w[2] not in onS:
                        weave_w(*w)
            if n + LEAD < UNITS and n != 2:
                for t in range(4):
                    logits(n + LEAD, t)
            if n + 1 < UNITS:
                for gg, kk in fill[n + 1]:
                    widen_w(gg, kk)
                    for j in onS:
                        weave_w(gg, kk, j, False)
            if n in (0, 1):
                widen_x(1, 2 * n, False)
                widen_x(1, 2 * n + 1, False)
            if n < UNITS - 2 :
                subtract(n, 0)
            if n + 1 < UNITS and n < UNITS - 2:
                turn_y(n + 1, 0)
            if n == 0:
                quant_w(0, 0)
                permute_u(3, 0)
            weave(0)
            if n < UNITS - 2:
                subtract(n, 1)
            weave(1)
            if n == 2:
                quant_x(1, 0)
                quant_x(1, 1)
                for t in range(4):
                    logits(n + LEAD, t)
            if NG <= n < UNITS:
                m = n - NG
                for q in (2 * m, 2 * m + 1):
                    k, i = divmod(q, 4)
                    gradient(0, i, k, range(NG), "o", 3)
                    store(0, i, k, False)
            if n + 1 < UNITS and n < UNITS - 2:
                turn_y(n + 1, 1)
            if n == 0:
                permute_u(3, 1)
                permute_us(3)
            if n in (0, 1):
                turn_x(1, n, 0)
                turn_x(1, n, 1)
            if n == UNITS - 3:
                scale_e(n, 0)
                subtract(n + 1, 0)
                turn_y(n + 2, 0)
                scale_e(n, 1)
                subtract(n + 1, 1)
                turn_y(n + 2, 1)
                weave(2)
                weave(3)
                for gg, kk in fill[n]:
                    quant_w(gg, kk)
                quant_e(n)
                continue
            if n == UNITS - 2:
                scale_e(n, 0)
                subtract(n + 1, 0, 0, 256)
                scale_e(n, 1)
                subtract(n + 1, 1, 0, 256)
                quant_e(n)
                continue
            if n == UNITS - 1:
                scale_e(n, 0)
                subtract(n, 0, 256, 512)
                subtract(n, 1, 256, 512)
                quant_e(n, 0, 256)
                scale_e(n, 1)
                quant_e(n, 256, 512)
                continue
            scale_e(n, 0)
            weave(2)
            scale_e(n, 1)
            weave(3)
            for gg, kk in fill[n]:
                quant_w(gg, kk)
            quant_e(n)

        n = UNITS - 1
        slots = [("o", 3), ("o", 3), ("o", 3), ("z", 3), ("z", 3), ("z", 3), ("y", 2), ("y", 2)]
        for i in range(4):
            for k in range(2):
                gradient(1, i, k, range(NG - 1), *slots[2 * i + k])
        for i in range(4):
            for k in range(2):
                gradient(1, i, k, [NG - 1], *slots[2 * i + k])
                store(1, i, k, k == 1)
